import numpy as np
import ml_dtypes


def mxq(x, axis, fmt="e4m3"):
    dtype, down = {"e4m3": (ml_dtypes.float8_e4m3fn, 7), "e5m2": (ml_dtypes.float8_e5m2, 14)}[fmt]
    v = np.moveaxis(np.asarray(x, np.float32).astype(ml_dtypes.bfloat16).astype(np.float64), axis, -1)
    blocks = v.reshape(v.shape[:-1] + (-1, 32))
    amax = np.abs(blocks).max(-1, keepdims=True)
    byte = np.maximum(np.where(amax > 0, np.frexp(amax)[1] - 1 + 127, 0) - down, 1)
    scale = np.exp2(byte - 127.0)
    codes = (blocks / scale).astype(np.float32).astype(dtype).astype(np.float64)
    return np.moveaxis((codes * scale).reshape(v.shape), -1, axis)


WIDE = False


def mx_kscale(k):
    if not WIDE:
        return np.ones(k)
    levels = np.array([10, -10, 5, -5, 0])
    if k % 512:
        return np.exp2(np.random.permutation(np.resize(levels, k // 32))).repeat(32)
    a = np.empty((k // 512, 16))
    for p in range(k // 512):
        a[p, :8] = np.random.permutation(np.resize(levels, 8))
        for g in range(8):
            far = levels[np.abs(levels - a[p, g]) >= 10]
            a[p, g + 8] = far[np.random.randint(len(far))]
    return np.exp2(a.ravel()).repeat(32)


BF16 = ml_dtypes.bfloat16


def bf(x):
    return np.asarray(x, np.float32).astype(BF16)


def f64(x):
    return np.asarray(x).astype(np.float64)


B, DA, DV, ACT, Z = 2048, 1024, 512, 8, 128


def setup_inputs():
    sa = mx_kscale(DA)
    sv = mx_kscale(DV)
    u = mx_kscale(B)
    return {"ha": bf(np.random.standard_normal((B, DA)) * sa),
            "wa": bf(np.random.standard_normal((DA, ACT * Z)) / np.sqrt(DA) / sa[:, None]),
            "ba": bf(0.5 * np.random.standard_normal((ACT, Z))),
            "hv": bf(np.random.standard_normal((B, DV)) * sv),
            "wv": bf(np.random.standard_normal((DV, Z)) / np.sqrt(DV) / sv[:, None]),
            "bv": bf(0.5 * np.random.standard_normal(Z)),
            "y": bf(np.random.standard_normal((B, ACT, Z))),
            "tau": bf(np.random.uniform(0.05, 0.95, Z)),
            "c": bf(np.random.uniform(0.5, 1.5, B) * u),
            "ea": bf(np.random.standard_normal((B, DA)) / np.sqrt(B) / u[:, None]),
            "ev": bf(np.random.standard_normal((B, DV)) / np.sqrt(B) / u[:, None])}


def reference(ha, wa, ba, hv, wv, bv, y, tau, c, ea, ev):
    adv = (mxq(f64(ha), 1, "e4m3") @ mxq(f64(wa), 0, "e4m3")).reshape(B, ACT, Z) + f64(ba)[None, :, :]
    val = (mxq(f64(hv), 1, "e4m3") @ mxq(f64(wv), 0, "e4m3")) + f64(bv)[None, :]
    q = val[:, None, :] + adv - adv.mean(axis=1, keepdims=True)
    d = f64(y) - q
    tq = f64(tau)[None, None, :]
    g = np.where(d > 0, tq, 1.0 - tq) * np.tanh(d) * f64(c)[:, None, None]
    ga = (g - g.mean(axis=1, keepdims=True)).reshape(B, ACT * Z)
    gv = g.sum(axis=1)
    dwa = mxq(f64(ea), 0, "e4m3").T @ mxq(ga, 0, "e4m3")
    dwv = mxq(f64(ev), 0, "e4m3").T @ mxq(gv, 0, "e4m3")
    return dwa, dwv

from contextlib import ExitStack

import concourse.mybir as mybir
from concourse.masks import make_identity

B, DA, DV, ACT, Z = 2048, 1024, 512, 8, 128
N_OUT = ACT * Z
FLOPS = 2 * 2 * B * (DA * N_OUT + DV * Z)

F32 = mybir.dt.float32
BF16 = mybir.dt.bfloat16
U32 = mybir.dt.uint32
U8 = mybir.dt.uint8
FP8X4 = mybir.dt.float8_e4m3fn_x4
ALU = mybir.AluOpType
ACTF = mybir.ActivationFunctionType
AXIS = mybir.AxisListType

P = 128
PACK = 4
K_PASS = P * PACK
BANK = 512
CHUNKS = B // K_PASS
HALVES = N_OUT // BANK
PER_HALF = ACT // HALVES
PIECE = 256
BV_ROW, TAU_ROW = 8, 9
ON_SCALAR = [(), (), (), ()]
FREE_TAGS = ["turn", "turn", "adv", "adv", "adv", "diff", "diff"]
PARKED = [(m, 1) for m in range(ACT - 5, ACT)]

ORDER = """
load_wa,0,0 wa_piece,0,0,s load_ha,0,0 wa_piece,0,1,v load_ha,0,1 load_ha,0,2 load_ha,0,3 turn,0,0
turn_out,0,0,s turn,0,1 turn_out,0,1,v turn,0,2 turn_out,0,2,s turn,0,3 turn_out,0,3,s turn_rows quant_wa,0,0
quant_h,0,0 load_hv,0 turn,0,4 turn,0,5 turn_out,0,4,s load_wa,0,1 wa_piece,0,2,v wa_piece,0,3,v
turn_out,0,5,s load_ha,1,0 load_ha,1,1 turn,1,0 turn_out,1,0,s quant_h,0,1 quant_wa,0,1 mean_passes,0,0
mean_passes,0,1 constants,0 load_wa,1,0 constants,1 wa_piece,1,0,v quant_h,0,2 wa_piece,1,1,s quant_wa,1,0
load_ha,1,2 load_ha,1,3 turn,1,1 turn_out,1,1,s turn,1,2 turn,1,3 turn_out,1,3,s load_wa,1,1 wa_piece,1,2,v
wa_piece,1,3,v quant_wa,1,1 mean_passes,0,2 load_wv wv_piece turn_out,1,2,v quant_wv mean_passes,0,3
mean_passes,0,4 mean_out,0,s load_y,0,0 load_ea,0 ea_piece,0,1,s ea_piece,0,0,s ea_piece,0,3,s ea_piece,0,2,v
constants,2 adv,0,0 neg_q,0,0 adv,0,1 adv,0,2 neg_q,0,1 adv,0,3 adv,0,4 neg_q,0,2 adv,0,5 neg_q,0,3 neg_q,0,4
adv,0,6 adv,0,7 neg_q,0,5 neg_q,0,6 neg_q,0,7 load_ha,2,0 diff,0,0,0 tanh,0,0,0 load_y,0,1 load_y,0,2
load_ha,2,1 load_ha,2,2 load_ha,2,3 diff,0,0,1 tanh,0,0,1 absolute,0,0 load_ha,3,0 load_y,0,3 load_hv,1
load_ha,3,1 load_ea,1 turn,1,4 turn,1,5 diff,0,1,0 diff,0,1,1 tanh,0,1,0 quant_ea,0,1 quant_ea,0,0 quant_h,1,1
turn_out,1,4,v turn,2,0 turn_out,1,5,v quant_h,1,2 turn,2,1 tanh,0,1,1 diff,0,2,0 diff,0,2,1 absolute,0,1
quant_h,1,0 mean_passes,1,0 mean_passes,1,1 mean_passes,1,2 mean_passes,1,3 mean_passes,1,4 turn_out,2,0,s
tanh,0,2,0 tanh,0,2,1 turn,2,2 diff,0,3,0 diff,0,3,1 weigh,0,0 weigh,0,1 combine,0,0 combine,0,1
ea_piece,1,1,s absolute,0,2 weigh,0,2 ea_piece,1,2,v combine,0,2 ea_piece,1,0,s quant_ea,1,0 adv,1,0
mean_out,1,s neg_q,1,0 adv,1,1 neg_q,1,1 adv,1,2 neg_q,1,2 adv,1,3 neg_q,1,3 adv,1,4 neg_q,1,4 adv,1,5 adv,1,6
ea_piece,1,3,s quant_ea,1,1 neg_q,1,5 load_ev,0 load_y,1,0 load_ea,2 load_hv,2 adv,1,7 turn_out,2,1,s
quant_h,2,0 tanh,0,3,0 turn_out,2,2,s ev_piece,0,1,s tanh,0,3,1 absolute,0,3 weigh,0,3 combine,0,3 neg_q,1,6
neg_q,1,7 sum_actions,0,0 turn,2,3 turn,2,4 load_ha,3,2 load_ha,3,3 sum_actions,0,1 load_ea,3 load_y,1,1
turn_out,2,3,s turn,2,5 load_hv,3 turn_out,2,4,s turn_out,2,5,s load_y,1,2 load_y,1,3 load_y,2,0
sum_actions,0,2 sum_actions,0,3 sum_out,0,s diff,1,0,0 tanh,1,0,0 turn_back,0 diff,1,0,1 tanh,1,0,1
ev_piece,0,0,s mean_passes,2,0 diff,1,1,0 tanh,1,1,0 diff,1,1,1 tanh,1,1,1 absolute,1,0 absolute,1,1 turn,3,0
diff,1,2,0 diff,1,2,1 tanh,1,2,0 turn_out,3,0,s turn,3,1 quant_h,2,1 mean_passes,2,1 turn_out,3,1,s tanh,1,2,1
absolute,1,2 mean_passes,2,2 mean_passes,2,3 quant_h,2,2 mean_passes,2,4 ea_piece,2,0,s mean_out,2,s
centre,0,0 centre,0,1 weigh,1,0 weigh,1,1 diff,1,3,0 diff,1,3,1 turn,3,2 gv_out,0,s turn_out,3,2,s tanh,1,3,1
ea_piece,3,1,s quant_ga,0,0 combine,1,0 quant_ga,0,1 tanh,1,3,0 absolute,1,3 combine,1,1 weigh,1,2 load_y,2,1
load_y,2,2 load_ev,2 adv,2,0 adv,2,1 neg_q,2,0 neg_q,2,1 adv,2,2 adv,2,3 adv,2,4 neg_q,2,2 neg_q,2,3 neg_q,2,4
adv,2,5 adv,2,6 adv,2,7 neg_q,2,5 neg_q,2,6 diff,2,0,0 tanh,2,0,0 neg_q,2,7 load_y,2,3 load_y,3,0 diff,2,0,1
load_y,3,1 tanh,2,0,1 quant_h,3,0 combine,1,2 weigh,1,3 turn,3,3 turn_out,3,3,s quant_h,3,1 absolute,2,0
weigh,2,0 sum_actions,1,0 diff,2,1,0 tanh,2,1,0 diff,2,1,1 tanh,2,1,1 absolute,2,1 load_y,3,2 sum_actions,1,1
diff,2,2,0 turn,3,4 turn,3,5 turn_out,3,4,s turn_out,3,5,s combine,1,3 sum_actions,1,2 sum_actions,1,3
combine,2,0 weigh,2,1 quant_h,3,2 diff,2,2,1 tanh,2,2,0 diff,2,3,0 sum_out,1,s turn_back,1 centre,1,0
tanh,2,2,1 absolute,2,2 ea_piece,2,2,s mean_passes,3,0 adv,3,0 mean_passes,3,1 diff,2,3,1 tanh,2,3,0
mean_passes,3,2 mean_passes,3,3 mean_passes,3,4 adv,3,1 weigh,2,2 combine,2,1 quant_gv,0 centre,1,1
ea_piece,3,3,s mean_out,3,s tanh,2,3,1 neg_q,3,0 adv,3,2 adv,3,3 neg_q,3,1 adv,3,4 neg_q,3,2 adv,3,5
gv_out,1,s absolute,2,3 ea_piece,2,3,s neg_q,3,3 adv,3,6 neg_q,3,4 adv,3,7 weigh,2,3 combine,2,2 combine,2,3
quant_gv,1 load_ev,1 ev_piece,1,0,s diff,3,0,0 ev_piece,1,1,s tanh,3,0,0 load_y,3,3 load_ev,3 neg_q,3,5
neg_q,3,6 neg_q,3,7 sum_actions,2,0 sum_actions,2,1 sum_actions,2,2 sum_actions,2,3 sum_out,2,s turn_back,2
ea_piece,2,1,s quant_ga,1,0 centre,2,0 quant_ga,1,1 centre,2,1 diff,3,0,1 tanh,3,0,1 diff,3,1,0 tanh,3,1,0
quant_ea,2,1 quant_ga,2,1 absolute,3,0 weigh,3,0 diff,3,1,1 tanh,3,1,1 diff,3,2,0 tanh,3,2,0 absolute,3,1
diff,3,2,1 diff,3,3,0 tanh,3,2,1 tanh,3,3,0 diff,3,3,1 ev_piece,3,1,s tanh,3,3,1 gv_out,2,s absolute,3,2
ea_piece,3,0,s dwa_passes,5,1,0,3,2 dwa_passes,6,1,0,3,3 dwa_passes,7,1,0,3,4 park,5,1,s quant_ea,2,0
dwa_passes,3,1,0,3,0 dwa_passes,4,1,0,3,1 combine,3,0 sum_actions,3,0 weigh,3,1 quant_ga,2,0
dwa_passes,5,0,0,3,5 dwa_passes,6,0,0,3,6 absolute,3,3 ev_piece,2,1,s park,6,1,s combine,3,1
dwa_passes,2,0,0,3,2 sum_actions,3,1 weigh,3,2 weigh,3,3 combine,3,2 sum_actions,3,2 combine,3,3
sum_actions,3,3 ea_piece,3,2,s sum_out,3,s turn_back,3 park,3,1,s dwa_passes,0,0,0,3,0 quant_gv,2 quant_ea,3,0
park,4,1,v quant_ea,3,1 dwa_passes,1,0,0,3,1 ev_piece,3,0,s park,7,1,s ev_piece,2,0,s dwa_passes,3,0,0,3,3
dwa_passes,4,0,0,3,4 centre,3,0 quant_ga,3,0 dwa_passes,0,0,3,4,-1 dwa_out,0,0,s dwa_store,0,0
dwa_passes,1,0,3,4,-1 dwa_out,1,0,s dwa_passes,2,0,3,4,-1 dwa_out,2,0,s dwa_store,1,0 dwa_store,2,0
dwa_passes,3,0,3,4,-1 dwa_out,3,0,s dwa_passes,5,0,3,4,-1 dwa_passes,4,0,3,4,-1 dwa_out,4,0,s dwa_store,3,0
dwa_store,4,0 dwa_passes,6,0,3,4,-1 dwa_out,5,0,s dwa_out,6,0,s dwa_store,5,0 dwa_passes,7,0,0,4,0
dwa_store,6,0 centre,3,1 quant_ev,3 quant_ga,3,1 dwa_passes,4,1,3,4,2 quant_ev,1 dwa_passes,7,1,3,4,5
dwa_passes,5,1,3,4,3 dwa_passes,0,1,0,4,6 dwa_out,7,0,s dwa_out,0,1,s dwa_add,7,1 dwa_store,7,1 dwa_store,7,0
dwa_passes,3,1,3,4,1 dwa_passes,6,1,3,4,4 dwa_add,4,1 dwa_add,5,1 dwa_store,5,1 dwa_store,4,1 gv_out,3,s
dwa_store,0,1 dwa_passes,1,1,0,4,0 dwa_out,1,1,s dwa_store,1,1 dwa_add,3,1 dwa_passes,2,1,0,4,1 dwa_out,2,1,s
dwa_store,3,1 quant_ev,0 quant_ev,2 dwa_add,6,1 quant_gv,3 dwa_store,6,1 dwa_store,2,1 dwv_passes dwv_out,s
dwv_store
"""


def tile_dueling_quantile_trace_update_f4_kernel(
    tc, ha, wa, ba, hv, wv, bv, y, tau, c, ea, ev, out_0, out_1
):
    nc = tc.nc
    ha_rows = ha.rearrange("(j p t) k -> j p t k", p=P, t=PACK)
    hv_rows = hv.rearrange("(j p t) k -> j p t k", p=P, t=PACK)
    y_rows = y.rearrange("(j p t) a z -> j p t (a z)", p=P, t=PACK)
    wa_rows = wa.rearrange("(g p t) n -> g p t n", p=P, t=PACK)
    ea_rows = ea.rearrange("(j p t) n -> j p t n", p=P, t=PACK)
    ev_rows = ev.rearrange("(j p t) n -> j p t n", p=P, t=PACK)

    with ExitStack() as ctx:
        keep = ctx.enter_context(tc.tile_pool(name="keep", bufs=1))
        work = ctx.enter_context(tc.tile_pool(name="work", bufs=1))
        psum = ctx.enter_context(tc.psum_pool(name="psum", bufs=1))
        ctx.enter_context(tc.manual_schedule())

        bank_bufs = {"turn": 2, "adv": 3, "diff": 2, "sum": 1}

        def new_bank(tag, dtype=F32):
            return psum.tile([P, BANK], dtype, name=tag, tag=tag, bufs=bank_bufs[tag])

        def mx_tiles(name, width):
            codes = keep.tile([P, width], U32, name=name + "_codes", align_bytes=64)
            scales = keep.tile([P, width], U8, name=name + "_scales", align_bytes=64)
            return codes, scales

        def quantize(mx, col0, grouped):
            width = grouped.shape[1] // PACK
            cols = slice(col0, col0 + width)
            nc.vector.quantize_mx(out=mx[0][:, cols].bitcast(FP8X4), scales=mx[1][:, cols], in_=grouped)

        def mx_pass(acc, lhs, lhs_col, rhs, rhs_col, start, stop):
            m = slice(lhs_col, lhs_col + P)
            n = slice(rhs_col, rhs_col + acc.shape[1])
            nc.tensor.matmul_mx(
                out=acc,
                lhsT=lhs[0][:, m].bitcast(FP8X4),
                lhsT_scale=lhs[1][:, m],
                rhs=rhs[0][:, n].bitcast(FP8X4),
                rhs_scale=rhs[1][:, n],
                start=start,
                stop=stop,
            )

        def move(eng, dst, src):
            if eng == "v":
                nc.vector.tensor_copy(out=dst, in_=src)
            elif eng == "s":
                nc.scalar.copy(out=dst, in_=src)
            else:
                nc.gpsimd.tensor_scalar(out=dst, in0=src, scalar1=1.0, scalar2=0.0, op0=ALU.mult, op1=ALU.add)

        def scale_out(eng, dst, src, factor):
            if eng == "v":
                nc.vector.tensor_scalar(out=dst, in0=src, scalar1=factor, scalar2=None, op0=ALU.mult)
            else:
                nc.scalar.activation(dst, src, ACTF.Copy, scale=factor)

        def interleave_views(raw, grouped, c0, c1):
            src = raw[:, :, c0:c1].rearrange("p t (c i) -> p c t i", i=PACK)
            dst = grouped[:, PACK * c0 : PACK * c1].rearrange("p (c i t) -> p c t i", i=PACK, t=PACK)
            return dst, src

        wa_mx = mx_tiles("wa", 2 * N_OUT)
        wv_mx = mx_tiles("wv", Z)
        h_mx = mx_tiles("h", 3 * K_PASS)
        ea_mx = mx_tiles("ea", CHUNKS * DA)
        ev_mx = mx_tiles("ev", CHUNKS * DV)
        ga_mx = mx_tiles("ga", CHUNKS * N_OUT)
        gv_mx = mx_tiles("gv", CHUNKS * Z)
        ident_f = keep.tile([P, P], F32, name="ident_f")
        ident_b = keep.tile([P, P], BF16, name="ident_b")
        rows = keep.tile([P, Z], BF16, name="rows")
        tau_c = keep.tile([P, Z], F32, name="tau_c")
        neg_bias = keep.tile([P, ACT], F32, name="neg_bias")
        stat = keep.tile([P, 2], F32, name="stat")
        c_raw = keep.tile([P, CHUNKS, PACK], BF16, name="c_raw")
        c_full = keep.tile([P, CHUNKS * PACK], F32, name="c_full")
        c_half = keep.tile([P, CHUNKS * PACK], F32, name="c_half")
        warm = keep.tile([P, 1], F32, name="warm")
        h_grouped = keep.tile([P, 3 * K_PASS * PACK], BF16, name="h_grouped", align_bytes=64)

        t = {}

        def load(key, tag, bufs, src):
            tile = work.tile(list(src.shape), BF16, name=tag, tag=tag, bufs=bufs)
            nc.sync.dma_start(out=tile[:], in_=src)
            t[key] = tile

        def load_ha(j, s):
            load(("ha", j, s), "ha_raw", 6, ha_rows[j, :, s, :])

        def load_hv(j):
            load(("hv", j), "hv_raw", 1, hv_rows[j])

        def load_y(j, s):
            load(("y", j, s), "y_raw", 5, y_rows[j, :, s, :])

        def load_wide(key, src, h):
            if key not in t:
                t[key] = work.tile([P, PACK, DA], BF16, name="wide_raw", tag="wide_raw", bufs=2)
            cols = slice(h * BANK, (h + 1) * BANK)
            nc.sync.dma_start(out=t[key][:, :, cols], in_=src[:, :, cols])

        def load_wa(g, h):
            load_wide(("wa", g), wa_rows[g], h)

        def load_ea(j):
            load(("ea", j), "wide_raw", 2, ea_rows[j])

        def load_ev(j):
            load(("ev", j), "ev_raw" if j % 2 == 0 else "hv_raw", 1, ev_rows[j])

        def load_wv():
            load(("wv",), "wv_raw", 1, wv.rearrange("(p t) z -> p t z", t=PACK))

        def grouped(key, tag, bufs, width):
            if key not in t:
                t[key] = work.tile([P, PACK * width], BF16, name=tag, tag=tag, bufs=bufs, align_bytes=64)
            return t[key][:]

        def turn(j, i):
            g, pair = divmod(i, 2)
            acc = new_bank("turn")
            t[("turn", j, i)] = acc
            for s2 in range(2):
                s = 2 * pair + s2
                src = t[("ha", j, s)][:] if g < 2 else t[("hv", j)][:, s, :]
                words = src.bitcast(F32)
                w0 = (g % 2) * 2 * P
                for u in range(2):
                    q = 2 * s2 + u
                    nc.tensor.transpose(acc[:, q * P : (q + 1) * P], words[:, w0 + u : w0 + 2 * P : 2], ident_f[:])

        def turn_out(j, i, eng):
            lo = i * 2 * P * PACK
            dst = h_grouped[:, lo : lo + 2 * P * PACK].bitcast(F32).rearrange("p (s r u) -> p s r u", s=2, u=2)
            move(eng, dst, t[("turn", j, i)][:].rearrange("p (s u r) -> p s r u", s=2, u=2))

        def quant_h(j, g):
            quantize(h_mx, g * K_PASS, h_grouped[:, PACK * g * K_PASS : PACK * (g + 1) * K_PASS])

        def mean_passes(j, i):
            if i == 0:
                t[("mean_acc", j)] = new_bank("adv")
            acc = t[("mean_acc", j)]
            if i < 4:
                g, h = divmod(i, 2)
                for a in range(h * PER_HALF, (h + 1) * PER_HALF):
                    mx_pass(acc[:], wa_mx, g * N_OUT + a * Z, h_mx, g * K_PASS, i == 0 and a == 0, False)
            else:
                mx_pass(acc[:], wv_mx, 0, h_mx, 2 * K_PASS, False, True)

        def mean_out(j, eng):
            t[("mean", j)] = work.tile([P, BANK], F32, name="mean", tag="mean", bufs=1)
            scale_out(eng, t[("mean", j)][:], t[("mean_acc", j)][:], 1.0 / ACT)

        def adv(j, a):
            acc = new_bank("adv")
            t[("adv", j, a)] = acc
            for g in range(2):
                mx_pass(acc[:], wa_mx, g * N_OUT + a * Z, h_mx, g * K_PASS, g == 0, g == 1)

        def neg_q(j, a):
            tile = work.tile([P, BANK], F32, name="nq", tag="nq", bufs=ACT)
            t[("nq", j, a)] = tile
            if a in ON_SCALAR[j]:
                nc.scalar.activation(tile[:], t[("adv", j, a)][:], ACTF.Identity, bias=neg_bias[:, a : a + 1], scale=-1.0)
            else:
                nc.vector.scalar_tensor_tensor(
                    out=tile[:], in0=t[("mean", j)][:], scalar=neg_bias[:, a : a + 1], in1=t[("adv", j, a)][:],
                    op0=ALU.add, op1=ALU.subtract,
                )

        def diff(j, s, h):
            acc = new_bank("diff")
            t[("diff", j, s, h)] = acc
            nc.tensor.matmul(acc[:], lhsT=ident_b[:], rhs=t[("y", j, s)][:, h * BANK : (h + 1) * BANK], start=True, stop=False)
            terms = []
            for i in range(PER_HALF):
                a = h * PER_HALF + i
                terms.append((i, t[("nq", j, a)]))
                if a in ON_SCALAR[j]:
                    terms.append((i, t[("mean", j)]))
            for n, (i, src) in enumerate(terms):
                nc.tensor.matmul(
                    acc[:, i * Z : (i + 1) * Z], lhsT=src[:, s * P : (s + 1) * P],
                    rhs=ident_f[:], is_transpose=True, start=False, stop=n == len(terms) - 1,
                )

        def tanh(j, s, h):
            if ("g", j) not in t:
                t[("g", j)] = work.tile([P, PACK, N_OUT], F32, name="g", tag="g", bufs=2)
            nc.scalar.activation(t[("g", j)][:, s, h * BANK : (h + 1) * BANK], t[("diff", j, s, h)][:], ACTF.Tanh)

        def absolute(j, s):
            t[("abs", j, s)] = work.tile([P, N_OUT], F32, name="mag", tag="mag", bufs=3)
            nc.scalar.activation(t[("abs", j, s)][:], t[("g", j)][:, s, :], ACTF.Abs)

        def weigh(j, s):
            mag = t[("abs", j, s)][:].rearrange("p (a z) -> p a z", a=ACT)
            col = j * PACK + s
            nc.vector.scalar_tensor_tensor(
                out=mag, in0=mag, scalar=c_full[:, col : col + 1],
                in1=tau_c[:].unsqueeze(1).broadcast_to([P, ACT, Z]), op0=ALU.mult, op1=ALU.mult,
            )

        def combine(j, s):
            g_s = t[("g", j)][:, s, :]
            col = j * PACK + s
            nc.vector.scalar_tensor_tensor(
                out=g_s, in0=g_s, scalar=c_half[:, col : col + 1], in1=t[("abs", j, s)][:], op0=ALU.mult, op1=ALU.add,
            )

        def sum_actions(j, s):
            if ("sum_acc", j) not in t:
                t[("sum_acc", j)] = new_bank("sum")
            for a in range(ACT):
                nc.tensor.matmul(
                    t[("sum_acc", j)][:, s * P : (s + 1) * P], lhsT=t[("g", j)][:, s, a * Z : (a + 1) * Z],
                    rhs=ident_f[:], is_transpose=True, start=a == 0, stop=a == ACT - 1,
                )

        def sum_out(j, eng):
            t[("sum", j)] = work.tile([P, BANK], F32, name="gsum", tag="gsum", bufs=1)
            scale_out(eng, t[("sum", j)][:], t[("sum_acc", j)][:], 1.0 / ACT)

        def turn_back(j):
            acc = new_bank("sum")
            t[("gmean", j)] = acc
            for s in range(PACK):
                nc.tensor.transpose(acc[:, s * Z : (s + 1) * Z], t[("sum", j)][:, s * P : (s + 1) * P], ident_f[:])

        def centre(j, h):
            g_h = t[("g", j)][:, :, h * BANK : (h + 1) * BANK].rearrange("p t (a z) -> p a z t", z=Z)
            mean = t[("gmean", j)][:].rearrange("p (t z) -> p z t", t=PACK).unsqueeze(1).broadcast_to([P, PER_HALF, Z, PACK])
            dst = grouped(("ga", j, h), "ga_grouped", 2, BANK).rearrange("p (a z t) -> p a z t", z=Z, t=PACK)
            nc.vector.tensor_tensor(out=dst, in0=g_h, in1=mean, op=ALU.subtract)

        def gv_out(j, eng):
            dst = grouped(("gv", j), "gv_grouped", 1, Z).rearrange("p (z t) -> p z t", t=PACK)
            scale_out(eng, dst, t[("gmean", j)][:].rearrange("p (t z) -> p z t", t=PACK), float(ACT))

        def quant_ga(j, h):
            quantize(ga_mx, j * N_OUT + h * BANK, t[("ga", j, h)][:])

        def quant_gv(j):
            quantize(gv_mx, j * Z, t[("gv", j)][:])

        def wa_piece(g, i, eng):
            views = interleave_views(t[("wa", g)][:], grouped(("wa_g", g), "wide_grouped", 2, DA), i * PIECE, (i + 1) * PIECE)
            move(eng, *views)

        def quant_wa(g, h):
            quantize(wa_mx, g * N_OUT + h * BANK, t[("wa_g", g)][:, h * BANK * PACK : (h + 1) * BANK * PACK])

        def wv_piece():
            dst, src = interleave_views(t[("wv",)][:], grouped(("wv_g",), "gv_grouped", 1, Z), 0, Z)
            nc.vector.tensor_scalar(out=dst, in0=src, scalar1=-float(ACT), scalar2=None, op0=ALU.mult)

        def quant_wv():
            quantize(wv_mx, 0, t[("wv_g",)][:])

        def ea_piece(j, i, eng):
            views = interleave_views(t[("ea", j)][:], grouped(("ea_g", j), "wide_grouped", 2, DA), i * PIECE, (i + 1) * PIECE)
            move(eng, *views)

        def ev_grouped(j):
            if j == 0:
                return grouped(("ev_g",), "ev_grouped", 1, DV)
            return h_grouped[:, (j - 1) * DV * PACK : j * DV * PACK]

        def ev_piece(j, i, eng):
            move(eng, *interleave_views(t[("ev", j)][:], ev_grouped(j), i * PIECE, (i + 1) * PIECE))

        def quant_ea(j, h):
            quantize(ea_mx, j * DA + h * BANK, t[("ea_g", j)][:, h * BANK * PACK : (h + 1) * BANK * PACK])

        def quant_ev(j):
            quantize(ev_mx, j * DV, ev_grouped(j))

        def dwa_passes(m, h, j0, j1, slot):
            if slot >= 0:
                t[("dwa", m, h)] = new_bank(FREE_TAGS[slot])
            last = CHUNKS - 2 if (m, h) in PARKED and j0 == 0 else CHUNKS - 1
            for j in range(j0, j1):
                mx_pass(t[("dwa", m, h)][:], ea_mx, j * DA + m * P, ga_mx, j * N_OUT + h * BANK, j == j0 and slot >= 0, j == last)

        def park(m, h, eng):
            if ("parked",) not in t:
                t[("parked",)] = work.tile([P, ACT, BANK], F32, name="parked", tag="g", bufs=2)
            move(eng, t[("parked",)][:, PARKED.index((m, h)), :], t[("dwa", m, h)][:])

        def dwa_out(m, h, eng):
            t[("res", m, h)] = work.tile([P, BANK], F32, name="nq", tag="nq", bufs=ACT)[:]
            move(eng, t[("res", m, h)], t[("dwa", m, h)][:])

        def dwa_add(m, h):
            part = t[("parked",)][:, PARKED.index((m, h)), :]
            t[("res", m, h)] = part
            nc.vector.tensor_tensor(out=part, in0=t[("dwa", m, h)][:], in1=part, op=ALU.add)

        def dwa_store(m, h):
            nc.sync.dma_start(out=out_0[m * P : (m + 1) * P, h * BANK : (h + 1) * BANK], in_=t[("res", m, h)])

        def dwv_passes():
            t[("dwv",)] = new_bank("sum")
            for m in range(DV // P):
                for j in range(CHUNKS):
                    mx_pass(t[("dwv",)][:, m * Z : (m + 1) * Z], ev_mx, j * DV + m * P, gv_mx, j * Z, j == 0, j == CHUNKS - 1)

        def dwv_out(eng):
            t[("res_v",)] = work.tile([P, BANK], F32, name="gsum", tag="gsum", bufs=1)
            move(eng, t[("res_v",)][:], t[("dwv",)][:])

        def dwv_store():
            nc.sync.dma_start(out=out_1.rearrange("(m p) z -> p m z", p=P), in_=t[("res_v",)][:].rearrange("p (m z) -> p m z", z=Z))

        def turn_rows():
            t[("rows_t",)] = new_bank("diff", BF16)
            nc.tensor.transpose(t[("rows_t",)][:, 0:P], rows[:], ident_b[:])
            t[("tau_acc",)] = new_bank("sum")
            nc.tensor.matmul(
                t[("tau_acc",)][:, 0:Z], lhsT=ident_b[:, TAU_ROW : TAU_ROW + 1].to_broadcast([P, P]), rhs=rows[:],
                start=True, stop=True,
            )

        def constants(i):
            rows_t = t[("rows_t",)]
            c_flat = c_raw[:].rearrange("p j t -> p (j t)")
            if i == 0:
                nc.vector.tensor_reduce(out=stat[:, 0:1], in_=rows_t[:, 0:ACT], axis=AXIS.X, op=ALU.add)
                nc.vector.tensor_scalar(out=tau_c[:], in0=t[("tau_acc",)][:, 0:Z], scalar1=-0.5, scalar2=None, op0=ALU.add)
            elif i == 1:
                nc.vector.scalar_tensor_tensor(
                    out=stat[:, 1:2], in0=stat[:, 0:1], scalar=1.0 / ACT, in1=rows_t[:, BV_ROW : BV_ROW + 1],
                    op0=ALU.mult, op1=ALU.subtract,
                )
                nc.vector.tensor_copy(out=c_full[:], in_=c_flat)
            else:
                nc.vector.tensor_scalar(
                    out=neg_bias[:], in0=rows_t[:, 0:ACT], scalar1=-1.0, scalar2=stat[:, 1:2], op0=ALU.mult, op1=ALU.add
                )
                nc.vector.tensor_scalar(out=c_half[:], in0=c_flat, scalar1=0.5, scalar2=None, op0=ALU.mult)

        steps = {
            "load_ha": load_ha, "load_hv": load_hv, "load_y": load_y, "load_wa": load_wa, "load_ea": load_ea,
            "load_ev": load_ev, "load_wv": load_wv, "turn": turn, "turn_out": turn_out, "quant_h": quant_h,
            "mean_passes": mean_passes, "mean_out": mean_out, "adv": adv, "neg_q": neg_q, "diff": diff, "tanh": tanh,
            "absolute": absolute, "weigh": weigh, "combine": combine, "sum_actions": sum_actions, "sum_out": sum_out,
            "turn_back": turn_back, "centre": centre, "gv_out": gv_out, "quant_ga": quant_ga, "quant_gv": quant_gv,
            "wa_piece": wa_piece, "quant_wa": quant_wa, "wv_piece": wv_piece, "quant_wv": quant_wv,
            "ea_piece": ea_piece, "ev_piece": ev_piece, "quant_ea": quant_ea, "quant_ev": quant_ev,
            "dwa_passes": dwa_passes, "park": park, "dwa_out": dwa_out, "dwa_add": dwa_add, "dwa_store": dwa_store,
            "dwv_passes": dwv_passes, "dwv_out": dwv_out, "dwv_store": dwv_store, "turn_rows": turn_rows,
            "constants": constants,
        }

        nc.vector.memset(rows[:], 0.0)
        nc.vector.memset(warm[:], 0.0)
        make_identity(nc, ident_f[:])
        make_identity(nc, ident_b[:])
        nc.scalar.dma_start(out=rows[0:ACT, :], in_=ba)
        nc.scalar.dma_start(out=rows[BV_ROW : BV_ROW + 1, :], in_=bv.unsqueeze(0))
        nc.scalar.dma_start(out=rows[TAU_ROW : TAU_ROW + 1, :], in_=tau.unsqueeze(0))
        nc.scalar.dma_start(out=c_raw[:], in_=c.rearrange("(j p t) -> p j t", p=P, t=PACK))
        nc.scalar.activation(warm[:], warm[:], ACTF.Tanh)

        for entry in ORDER.split():
            name, *args = entry.split(",")
            steps[name](*[arg if arg in ("v", "s", "g") else int(arg) for arg in args])
